import numpy as np
import ml_dtypes


def mxq(x, axis, fmt="e4m3"):
    dtype, down = {"e4m3": (ml_dtypes.float8_e4m3fn, 7), "e5m2": (ml_dtypes.float8_e5m2, 14)}[fmt]
    v = np.moveaxis(np.asarray(x, np.float32).astype(ml_dtypes.bfloat16).astype(np.float64), axis, -1)
    blocks = v.reshape(v.shape[:-1] + (-1, 32))
    amax = np.abs(blocks).max(-1, keepdims=True)
    byte = np.maximum(np.where(amax > 0, np.frexp(amax)[1] - 1 + 127, 0) - down, 1)
    scale = np.exp2(byte - 127.0)
    codes = (blocks / scale).astype(np.float32).astype(dtype).astype(np.float64)
    return np.moveaxis((codes * scale).reshape(v.shape), -1, axis)


WIDE = False


def mx_kscale(k):
    if not WIDE:
        return np.ones(k)
    levels = np.array([10, -10, 5, -5, 0])
    if k % 512:
        return np.exp2(np.random.permutation(np.resize(levels, k // 32))).repeat(32)
    a = np.empty((k // 512, 16))
    for p in range(k // 512):
        a[p, :8] = np.random.permutation(np.resize(levels, 8))
        for g in range(8):
            far = levels[np.abs(levels - a[p, g]) >= 10]
            a[p, g + 8] = far[np.random.randint(len(far))]
    return np.exp2(a.ravel()).repeat(32)


def f64(x):
    return np.asarray(x).astype(np.float64)


def striped(idx):
    return np.tile(idx.reshape(-1, 16).T, (8, 1)).astype(np.uint16)


def unstriped(offs):
    return offs[:16].T.reshape(-1).astype(np.int64)


E2M1 = np.array([0.0, 0.5, 1.0, 1.5, 2.0, 3.0, 4.0, 6.0, -0.0, -0.5, -1.0, -1.5, -2.0, -3.0, -4.0, -6.0])


def pack_weight(w, fmt):
    k, n = w.shape
    w = f64(np.asarray(w, np.float32).astype(ml_dtypes.bfloat16)).reshape(k // 32, 32, n)
    amax = np.abs(w).max(1)
    if fmt == "e4m3":
        byte = np.frexp(amax)[1] - 1 + 127 - 7
    else:
        mant, ex = np.frexp(amax / 6.0)
        byte = np.where(mant > 0.5, ex, ex - 1) + 127
    byte = np.clip(np.where(amax > 0, byte, 1), 1, 254)
    scaled = (w * np.exp2(127.0 - byte)[:, None, :]).reshape(k, n).astype(np.float32)
    by_word = np.ascontiguousarray(scaled.reshape(k // 512, 128, 4, n).transpose(0, 1, 3, 2))
    if fmt == "e4m3":
        words = by_word.astype(ml_dtypes.float8_e4m3fn).view(np.uint8)
    else:
        c = by_word.astype(ml_dtypes.float4_e2m1fn).view(np.uint8) & 0xF
        words = (c[..., 0::2] | (c[..., 1::2] << 4)).reshape(k // 512, 128, 2 * n)
    return np.ascontiguousarray(words), np.ascontiguousarray(byte.astype(np.uint8).reshape(k // 512, 16, n))


def unpack_weight(words, scales, fmt):
    g, _, n = scales.shape
    words = np.ascontiguousarray(words).reshape(g, 128, n, -1)
    if fmt == "e4m3":
        vals = words.view(ml_dtypes.float8_e4m3fn).astype(np.float64)
    else:
        nib = np.empty((g, 128, n, 4), np.uint8)
        nib[..., 0::2] = words & 0xF
        nib[..., 1::2] = words >> 4
        vals = E2M1[nib]
    vals = vals * np.repeat(np.exp2(scales.astype(np.float64) - 127.0), 8, axis=1)[..., None]
    return vals.transpose(0, 1, 3, 2).reshape(g * 512, n)


def gelu(v):
    return 0.5 * v * (1.0 + np.tanh(np.sqrt(2.0 / np.pi) * (v + 0.044715 * v**3)))


K, T, S, T2, P, H, N = 512, 4096, 1024, 2048, 1024, 1024, 768

def setup_inputs():
    n = np.random.standard_normal
    s = mx_kscale(K)[:, None]
    u = mx_kscale(H)[:, None]
    tab_words, tab_scales = pack_weight(n((K, T)) * s, "e4m3")
    w4_words, w4_scales = pack_weight(n((K, H)) / np.sqrt(K) / s, "e2m1")
    return {
        "tab_words": tab_words, "tab_scales": tab_scales,
        "offs": striped(np.random.permutation(T)[:S]),
        "w1": (n((K, H)) / np.sqrt(K) / s).astype(np.float32),
        "w4_words": w4_words, "w4_scales": w4_scales,
        "gain": (np.exp(0.3 * n(H)) * u[:, 0]).astype(np.float32),
        "page0": (n((H, T2)) * u).astype(np.float32),
        "wgs": np.exp(0.3 * n((128, S))).astype(np.float32),
        "offs2": striped(np.random.permutation(T2)[:S]),
        "offs3": striped(np.random.permutation(T2)[:P]),
        "offs4": striped(np.random.permutation(T2)[:P]),
        "w2": (n((H, N)) / np.sqrt(H) / u).astype(np.float32),
    }

def reference(tab_words, tab_scales, offs, w1, w4_words, w4_scales, gain, page0, wgs, offs2, offs3, offs4, w2):
    v = unpack_weight(tab_words, tab_scales, "e4m3")[:, unstriped(offs)]
    w4 = unpack_weight(w4_words, w4_scales, "e2m1")
    d1 = mxq(f64(w1), 0, "e4m3").T @ v
    d2 = w4.T @ v
    h = f64(gain)[:, None] * np.maximum(d1, d2)
    before = f64(page0)
    page = before.copy()
    page[:, unstriped(offs2)] = np.tile(f64(wgs), (H // 128, 1)) * h
    c = page[:, unstriped(offs3)]
    b = before[:, unstriped(offs4)]
    x = np.abs(c - b) + c
    return mxq(f64(w2), 0, "e4m3").T @ mxq(x, 0, "e4m3")

@@ -1,0 +1,267 @@
+from contextlib import ExitStack
+
+import concourse.mybir as mybir
+
+K, T, S, T2, M, H, N = 512, 4096, 1024, 2048, 1024, 1024, 768
+FLOPS = 2 * (2 * K * H * S + H * N * M)
+
+F32 = mybir.dt.float32
+BF16 = mybir.dt.bfloat16
+I32 = mybir.dt.int32
+U32 = mybir.dt.uint32
+U16 = mybir.dt.uint16
+U8 = mybir.dt.uint8
+FP8X4 = mybir.dt.float8_e4m3fn_x4
+FP4X4 = mybir.dt.float4_e2m1fn_x4
+ALU = mybir.AluOpType
+COPY = mybir.ActivationFunctionType.Copy
+
+P = 128
+PACK = 4
+PASSES = H // (P * PACK)
+SLICES = PASSES * PACK
+BANK = 512
+PIECES = (512, 256, 128, 128)
+
+
+def tile_list_tank_floor_repair_kernel(
+    tc, tab_words, tab_scales, offs, w1, w4_words, w4_scales, gain, page0, wgs, offs2, offs3, offs4, w2, out
+):
+    nc = tc.nc
+    with ExitStack() as ctx:
+        lists = ctx.enter_context(tc.tile_pool(name="lists", bufs=1))
+        keep = ctx.enter_context(tc.tile_pool(name="keep", bufs=1))
+        ring = ctx.enter_context(tc.tile_pool(name="ring", bufs=2))
+        psum = ctx.enter_context(tc.psum_pool(name="psum", bufs=1))
+        with tc.tile_pool(name="early", bufs=1) as early:
+
+            idx = lists.tile([P, S // 16], U16, name="idx")
+            idx2 = lists.tile([P, S // 16], U16, name="idx2")
+            idx3 = lists.tile([P, M // 16], U16, name="idx3")
+            idx4 = lists.tile([P, M // 16], U16, name="idx4")
+
+            tab_w = early.tile([P, T], U32, name="tab_w")
+            tab_s = early.tile([P, T], U8, name="tab_s")
+            w4_raw = early.tile([P, 2 * H], U8, name="w4_raw")
+            w4s_raw = early.tile([P, H], U8, name="w4s_raw")
+            w1_raw = [early.tile([P, PACK, 512], F32, name="w1_raw%d" % b) for b in range(PASSES)]
+            w2_raw = [early.tile([P, PACK, N], F32, name="w2_raw%d" % b) for b in range(PASSES)]
+
+            v_w = keep.tile([P, S], U32, name="v_w", align_bytes=64)
+            v_s = keep.tile([P, S], U8, name="v_s", align_bytes=64)
+            w4_c = [keep.tile([P, PACK * 2 * P], U8, name="w4_c%d" % b, align_bytes=64) for b in range(PASSES)]
+            w4_s = [keep.tile([P, PACK * P], U8, name="w4_s%d" % b, align_bytes=64) for b in range(PASSES)]
+            w1_c = [keep.tile([P, P], U32, name="w1_c%d" % s, align_bytes=64) for s in range(SLICES)]
+            w1_s = [keep.tile([P, P], U8, name="w1_s%d" % s, align_bytes=64) for s in range(SLICES)]
+            w2_c = [keep.tile([P, N], U32, name="w2_c%d" % b, align_bytes=64) for b in range(PASSES)]
+            w2_s = [keep.tile([P, N], U8, name="w2_s%d" % b, align_bytes=64) for b in range(PASSES)]
+            gains = keep.tile([P, PASSES, PACK], F32, name="gains")
+            wgs_t = [keep.tile([P, S], F32, name="wgs_t%d" % t) for t in range(PACK)]
+            pages = [keep.tile([P, T2], F32, name="page%d" % s) for s in range(SLICES)]
+            half_b = [keep.tile([P, PACK, M], F32, name="half_b%d" % b) for b in range(PASSES)]
+
+            page_rows = page0.rearrange("(b p t) c -> b t p c", p=P, t=PACK)
+            wgs_rows = wgs.rearrange("(q t) j -> t q j", t=PACK)
+
+            def load_page(s):
+                nc.sync.dma_start(out=pages[s][:], in_=page_rows[s // PACK, s % PACK])
+
+            def load_wgs(t):
+                for quad in (0, 2, 1, 3):
+                    nc.sync.dma_start(out=wgs_t[t][32 * quad : 32 * quad + 32, :], in_=wgs_rows[t])
+
+            def load_w1(b):
+                nc.sync.dma_start(out=w1_raw[b][:], in_=w1[:, 512 * b : 512 * (b + 1)].rearrange("(p j) c -> p j c", j=PACK))
+
+            def load_w2(b):
+                nc.sync.dma_start(out=w2_raw[b][:], in_=w2[512 * b : 512 * (b + 1), :].rearrange("(p t) n -> p t n", t=PACK))
+
+            nc.vector.memset(tab_s[:].bitcast(I32), 0)
+            nc.gpsimd.memset(w4s_raw[:].bitcast(I32), 0)
+            nc.sync.dma_start(idx[:], offs)
+            for quad in range(4):
+                nc.sync.dma_start(
+                    out=tab_s[32 * quad : 32 * quad + 4, :].bitcast(I32),
+                    in_=tab_scales[0, 4 * quad : 4 * quad + 4, :].bitcast(I32),
+                )
+            nc.sync.dma_start(out=tab_w[:].bitcast(I32), in_=tab_words[0].rearrange("p n i -> p (n i)").bitcast(I32))
+            nc.gpsimd.dma_start(out=w4_raw[:].bitcast(I32), in_=w4_words[0].bitcast(I32))
+            for quad in range(4):
+                nc.gpsimd.dma_start(
+                    out=w4s_raw[32 * quad : 32 * quad + 4, :].bitcast(I32),
+                    in_=w4_scales[0, 4 * quad : 4 * quad + 4, :].bitcast(I32),
+                )
+            nc.gpsimd.dma_start(out=gains[:], in_=gain.rearrange("(b p t) -> p b t", p=P, t=PACK))
+            nc.sync.dma_start(idx4[:], offs4)
+            load_page(0)
+            load_w1(0)
+            nc.sync.dma_start(idx2[:], offs2)
+            load_wgs(0)
+            load_page(1)
+            load_wgs(1)
+            load_w1(1)
+            load_w2(0)
+            load_page(2)
+            load_wgs(2)
+            load_w2(1)
+            load_page(3)
+            load_wgs(3)
+            nc.sync.dma_start(idx3[:], offs3)
+            for s in range(PACK, SLICES):
+                load_page(s)
+
+            def deal_w4(b):
+                nc.gpsimd.tensor_copy(
+                    out=w4_c[b][:].rearrange("p (t q e) -> p t q e", t=PACK, e=2),
+                    in_=w4_raw[:, 1024 * b : 1024 * (b + 1)].rearrange("p (q t e) -> p t q e", t=PACK, e=2),
+                )
+                nc.gpsimd.tensor_copy(
+                    out=w4_s[b][:].rearrange("p (t q) -> p t q", t=PACK),
+                    in_=w4s_raw[:, 512 * b : 512 * (b + 1)].rearrange("p (q t) -> p t q", t=PACK),
+                )
+
+            def prepare_w1(s):
+                b, t = divmod(s, PACK)
+                grouped = ring.tile([P, P, PACK], BF16, name="w1_grouped", align_bytes=64, bufs=4)
+                nc.scalar.copy(out=grouped[:], in_=w1_raw[b][:].rearrange("p j (q t) -> p t q j", t=PACK)[:, t])
+                nc.vector.quantize_mx(
+                    out=w1_c[s][:].bitcast(FP8X4), scales=w1_s[s][:], in_=grouped[:].rearrange("p q j -> p (q j)")
+                )
+
+            def prepare_w2(b):
+                raw = w2_raw[b]
+                for half in range(2):
+                    cols = slice(half * N // 2, (half + 1) * N // 2)
+                    grouped = early.tile([P, N // 2, PACK], BF16, name="w2_grouped", align_bytes=64, bufs=2)
+                    nc.scalar.copy(out=grouped[:], in_=raw[:, :, cols].rearrange("p t n -> p n t"))
+                    nc.vector.quantize_mx(
+                        out=w2_c[b][:, cols].bitcast(FP8X4), scales=w2_s[b][:, cols], in_=grouped[:].rearrange("p n t -> p (n t)")
+                    )
+
+            def stronger(s):
+                b, t = divmod(s, PACK)
+                strong = ring.tile([P, S], F32, name="strong", bufs=1)
+                for half in range(S // BANK):
+                    cols = slice(half * BANK, (half + 1) * BANK)
+                    d1 = psum.tile([P, BANK], F32, name="d1", bufs=2)
+                    d2 = psum.tile([P, BANK], F32, name="d2", bufs=2)
+                    nc.tensor.matmul_mx(
+                        out=d2[:],
+                        lhsT=w4_c[b][:, 2 * P * t : 2 * P * (t + 1)].bitcast(FP4X4),
+                        lhsT_scale=w4_s[b][:, P * t : P * (t + 1)],
+                        rhs=v_w[:, cols].bitcast(FP8X4),
+                        rhs_scale=v_s[:, cols],
+                        start=True,
+                        stop=True,
+                    )
+                    nc.tensor.matmul_mx(
+                        out=d1[:],
+                        lhsT=w1_c[s][:].bitcast(FP8X4),
+                        lhsT_scale=w1_s[s][:],
+                        rhs=v_w[:, cols].bitcast(FP8X4),
+                        rhs_scale=v_s[:, cols],
+                        start=True,
+                        stop=True,
+                    )
+                    d2_sb = ring.tile([P, BANK], F32, name="d2_sb")
+                    nc.scalar.copy(out=d2_sb[:], in_=d2[:])
+                    nc.vector.tensor_tensor(out=strong[:, cols], in0=d1[:], in1=d2_sb[:], op=ALU.max)
+                factor = ring.tile([P, S], F32, name="factor")
+                nc.scalar.activation(out=factor[:], in_=wgs_t[t][:], func=COPY, scale=gains[:, b, t : t + 1])
+                return strong, factor
+
+            def fetch_before(s):
+                b, t = divmod(s, PACK)
+                for half in range(2):
+                    nc.vector.tensor_scalar(
+                        half_b[b][:, t, 512 * half : 512 * (half + 1)],
+                        pages[s][:].indirect(idx4[:, 32 * half : 32 * (half + 1)]),
+                        0.5,
+                        0.0,
+                        ALU.mult,
+                        ALU.add,
+                    )
+
+            nc.vector.tensor_copy(v_s[:], tab_s[:].indirect(idx[:]))
+            nc.vector.tensor_copy(v_w[:], tab_w[:].indirect(idx[:]))
+            deal_w4(0)
+            fetch_before(0)
+            prepare_w1(0)
+            made = stronger(0)
+            for s in range(1, PACK):
+                prepare_w1(s)
+            deal_w4(1)
+            for s in range(SLICES):
+                strong, factor = made
+                nc.vector.tensor_tensor(pages[s][:].indirect(idx2[:]), strong[:], factor[:], ALU.mult)
+                if s + 1 < SLICES:
+                    made = stronger(s + 1)
+                    fetch_before(s + 1)
+                if s == 0:
+                    for later in range(PACK, SLICES):
+                        prepare_w1(later)
+                if s in (1, 2):
+                    prepare_w2(s - 1)
+
+        late = ctx.enter_context(tc.tile_pool(name="late", bufs=2))
+        out_rows = out.rearrange("(c p) m -> p c m", p=P)
+        steps = []
+        start = 0
+        for width in PIECES:
+            for b in range(PASSES):
+                steps.append((start, width, b))
+            start += width
+
+        def combine(start, width, b):
+            diff = late.tile([P, PACK, width], F32, name="diff")
+            for t in range(PACK):
+                nc.vector.tensor_tensor(
+                    diff[:, t, :],
+                    pages[PACK * b + t][:].indirect(idx3[:, start // 16 : (start + width) // 16]),
+                    half_b[b][:, t, start : start + width],
+                    ALU.subtract,
+                )
+            nc.vector.tensor_tensor(out=diff[:], in0=diff[:], in1=half_b[b][:, :, start : start + width], op=ALU.max)
+            grouped = late.tile([P, width, PACK], BF16, name="x_grouped", align_bytes=64)
+            nc.scalar.activation(out=grouped[:], in_=diff[:].rearrange("p t m -> p m t"), func=COPY, scale=2.0)
+            return grouped
+
+        def quantize_x(width, grouped):
+            codes = late.tile([P, width], U32, name="x_c", align_bytes=64, bufs=4)
+            scales = late.tile([P, width], U8, name="x_s", align_bytes=64, bufs=4)
+            nc.vector.quantize_mx(out=codes[:].bitcast(FP8X4), scales=scales[:], in_=grouped[:].rearrange("p m t -> p (m t)"))
+            return codes, scales
+
+        def score(start, width, operands, last):
+            per_bank = min(BANK // width, 3)
+            staged = late.tile([P, N // P, width], F32, name="staged")
+            for c0 in range(0, N // P, per_bank):
+                acc = psum.tile([P, per_bank, width], F32, name="acc", bufs=4)
+                for c in range(c0, c0 + per_bank):
+                    for b in range(PASSES):
+                        nc.tensor.matmul_mx(
+                            out=acc[:, c - c0, :],
+                            lhsT=w2_c[b][:, P * c : P * (c + 1)].bitcast(FP8X4),
+                            lhsT_scale=w2_s[b][:, P * c : P * (c + 1)],
+                            rhs=operands[b][0][:].bitcast(FP8X4),
+                            rhs_scale=operands[b][1][:],
+                            start=(b == 0),
+                            stop=(b == PASSES - 1),
+                        )
+                if last and (c0 // per_bank) % 2 == 1:
+                    nc.vector.tensor_copy(out=staged[:, c0 : c0 + per_bank, :], in_=acc[:])
+                else:
+                    nc.scalar.copy(out=staged[:, c0 : c0 + per_bank, :], in_=acc[:])
+                nc.sync.dma_start(out=out_rows[:, c0 : c0 + per_bank, start : start + width], in_=staged[:, c0 : c0 + per_bank, :])
+
+        operands = []
+        waiting = None
+        for step in steps + [None]:
+            grouped = combine(*step) if step is not None else None
+            if waiting is not None:
+                (w_start, w_width, w_b), w_grouped = waiting
+                operands.append(quantize_x(w_width, w_grouped))
+                if w_b == PASSES - 1:
+                    score(w_start, w_width, operands, step is None)
+                    operands = []
+            waiting = (step, grouped)

@@ -1,6 +1,7 @@
 from contextlib import ExitStack
 
 import concourse.mybir as mybir
+from concourse.masks import make_identity
 
 K, T, S, T2, M, H, N = 512, 4096, 1024, 2048, 1024, 1024, 768
 FLOPS = 2 * (2 * K * H * S + H * N * M)
@@ -15,13 +16,14 @@ FP8X4 = mybir.dt.float8_e4m3fn_x4
 FP4X4 = mybir.dt.float4_e2m1fn_x4
 ALU = mybir.AluOpType
 COPY = mybir.ActivationFunctionType.Copy
+RELU = mybir.ActivationFunctionType.Relu
 
 P = 128
 PACK = 4
 PASSES = H // (P * PACK)
 SLICES = PASSES * PACK
 BANK = 512
-PIECES = (512, 256, 128, 128)
+PIECES = (256, 256, 256, 128, 128)
 
 
 def tile_list_tank_floor_repair_kernel(
@@ -32,30 +34,29 @@ def tile_list_tank_floor_repair_kernel(
         lists = ctx.enter_context(tc.tile_pool(name="lists", bufs=1))
         keep = ctx.enter_context(tc.tile_pool(name="keep", bufs=1))
         ring = ctx.enter_context(tc.tile_pool(name="ring", bufs=2))
-        psum = ctx.enter_context(tc.psum_pool(name="psum", bufs=1))
-        with tc.tile_pool(name="early", bufs=1) as early:
+        with tc.tile_pool(name="early", bufs=1) as early, tc.psum_pool(name="psum", bufs=2) as psum:
 
             idx = lists.tile([P, S // 16], U16, name="idx")
             idx2 = lists.tile([P, S // 16], U16, name="idx2")
             idx3 = lists.tile([P, M // 16], U16, name="idx3")
             idx4 = lists.tile([P, M // 16], U16, name="idx4")
 
-            tab_w = early.tile([P, T], U32, name="tab_w")
+            tab_w = early.tile([P, T], U32, name="tab_w", tag="tab_w")
             tab_s = early.tile([P, T], U8, name="tab_s")
-            w4_raw = early.tile([P, 2 * H], U8, name="w4_raw")
+            w4_raw = [early.tile([P, H], U8, name="w4_raw%d" % b) for b in range(PASSES)]
             w4s_raw = early.tile([P, H], U8, name="w4s_raw")
-            w1_raw = [early.tile([P, PACK, 512], F32, name="w1_raw%d" % b) for b in range(PASSES)]
-            w2_raw = [early.tile([P, PACK, N], F32, name="w2_raw%d" % b) for b in range(PASSES)]
+            w1_raw = [early.tile([P, PACK, 512], F32, name="w1_raw%d" % b, tag="w1_raw%d" % b, align_bytes=64 if b == 0 else None) for b in range(PASSES)]
+            ident = early.tile([P, P], F32, name="ident")
+            x0_s = keep.tile([P, M], U8, name="x0_s", align_bytes=64)
 
             v_w = keep.tile([P, S], U32, name="v_w", align_bytes=64)
             v_s = keep.tile([P, S], U8, name="v_s", align_bytes=64)
             w4_c = [keep.tile([P, PACK * 2 * P], U8, name="w4_c%d" % b, align_bytes=64) for b in range(PASSES)]
             w4_s = [keep.tile([P, PACK * P], U8, name="w4_s%d" % b, align_bytes=64) for b in range(PASSES)]
-            w1_c = [keep.tile([P, P], U32, name="w1_c%d" % s, align_bytes=64) for s in range(SLICES)]
-            w1_s = [keep.tile([P, P], U8, name="w1_s%d" % s, align_bytes=64) for s in range(SLICES)]
-            w2_c = [keep.tile([P, N], U32, name="w2_c%d" % b, align_bytes=64) for b in range(PASSES)]
+            w1_c = [keep.tile([P, 512], U32, name="w1_c0", align_bytes=64)]
+            w1_s = keep.tile([P, H], U8, name="w1_s", align_bytes=64)
             w2_s = [keep.tile([P, N], U8, name="w2_s%d" % b, align_bytes=64) for b in range(PASSES)]
-            gains = keep.tile([P, PASSES, PACK], F32, name="gains")
+            gains = [keep.tile([P, PACK], F32, name="gains%d" % b) for b in range(PASSES)]
             wgs_t = [keep.tile([P, S], F32, name="wgs_t%d" % t) for t in range(PACK)]
             pages = [keep.tile([P, T2], F32, name="page%d" % s) for s in range(SLICES)]
             half_b = [keep.tile([P, PACK, M], F32, name="half_b%d" % b) for b in range(PASSES)]
@@ -70,81 +71,90 @@ def tile_list_tank_floor_repair_kernel(
                 for quad in (0, 2, 1, 3):
                     nc.sync.dma_start(out=wgs_t[t][32 * quad : 32 * quad + 32, :], in_=wgs_rows[t])
 
+            def load_gain(b):
+                nc.sync.dma_start(out=gains[b][:], in_=gain[512 * b : 512 * (b + 1)].rearrange("(p t) -> p t", t=PACK))
+
             def load_w1(b):
                 nc.sync.dma_start(out=w1_raw[b][:], in_=w1[:, 512 * b : 512 * (b + 1)].rearrange("(p j) c -> p j c", j=PACK))
 
-            def load_w2(b):
-                nc.sync.dma_start(out=w2_raw[b][:], in_=w2[512 * b : 512 * (b + 1), :].rearrange("(p t) n -> p t n", t=PACK))
-
             nc.vector.memset(tab_s[:].bitcast(I32), 0)
             nc.gpsimd.memset(w4s_raw[:].bitcast(I32), 0)
+            nc.sync.dma_start(idx4[:], offs4)
             nc.sync.dma_start(idx[:], offs)
+            nc.sync.dma_start(idx2[:], offs2)
+            nc.sync.dma_start(idx3[:], offs3)
+            load_gain(0)
+            for b in range(PASSES):
+                nc.sync.dma_start(out=w4_raw[b][:].bitcast(I32), in_=w4_words[0, :, H * b : H * (b + 1)].bitcast(I32))
+            load_page(0)
+            nc.sync.dma_start(out=tab_w[:].bitcast(I32), in_=tab_words[0].rearrange("p n i -> p (n i)").bitcast(I32))
             for quad in range(4):
                 nc.sync.dma_start(
                     out=tab_s[32 * quad : 32 * quad + 4, :].bitcast(I32),
                     in_=tab_scales[0, 4 * quad : 4 * quad + 4, :].bitcast(I32),
                 )
-            nc.sync.dma_start(out=tab_w[:].bitcast(I32), in_=tab_words[0].rearrange("p n i -> p (n i)").bitcast(I32))
-            nc.gpsimd.dma_start(out=w4_raw[:].bitcast(I32), in_=w4_words[0].bitcast(I32))
             for quad in range(4):
                 nc.gpsimd.dma_start(
                     out=w4s_raw[32 * quad : 32 * quad + 4, :].bitcast(I32),
                     in_=w4_scales[0, 4 * quad : 4 * quad + 4, :].bitcast(I32),
                 )
-            nc.gpsimd.dma_start(out=gains[:], in_=gain.rearrange("(b p t) -> p b t", p=P, t=PACK))
-            nc.sync.dma_start(idx4[:], offs4)
-            load_page(0)
             load_w1(0)
-            nc.sync.dma_start(idx2[:], offs2)
             load_wgs(0)
             load_page(1)
             load_wgs(1)
-            load_w1(1)
-            load_w2(0)
-            load_page(2)
             load_wgs(2)
-            load_w2(1)
-            load_page(3)
             load_wgs(3)
-            nc.sync.dma_start(idx3[:], offs3)
+            load_page(2)
+            load_gain(1)
+            load_page(3)
+            load_w1(1)
             for s in range(PACK, SLICES):
                 load_page(s)
 
             def deal_w4(b):
-                nc.gpsimd.tensor_copy(
-                    out=w4_c[b][:].rearrange("p (t q e) -> p t q e", t=PACK, e=2),
-                    in_=w4_raw[:, 1024 * b : 1024 * (b + 1)].rearrange("p (q t e) -> p t q e", t=PACK, e=2),
+                nc.vector.tensor_copy(
+                    out=w4_c[b][:].bitcast(U16).rearrange("p (t q) -> p t q", t=PACK),
+                    in_=w4_raw[b][:].bitcast(U16).rearrange("p (q t) -> p t q", t=PACK),
                 )
                 nc.gpsimd.tensor_copy(
                     out=w4_s[b][:].rearrange("p (t q) -> p t q", t=PACK),
                     in_=w4s_raw[:, 512 * b : 512 * (b + 1)].rearrange("p (q t) -> p t q", t=PACK),
                 )
 
-            def prepare_w1(s):
-                b, t = divmod(s, PACK)
-                grouped = ring.tile([P, P, PACK], BF16, name="w1_grouped", align_bytes=64, bufs=4)
-                nc.scalar.copy(out=grouped[:], in_=w1_raw[b][:].rearrange("p j (q t) -> p t q j", t=PACK)[:, t])
-                nc.vector.quantize_mx(
-                    out=w1_c[s][:].bitcast(FP8X4), scales=w1_s[s][:], in_=grouped[:].rearrange("p q j -> p (q j)")
+            def group_w1(s0, s1, grouped):
+                b, t0 = divmod(s0, PACK)
+                nc.scalar.copy(
+                    out=grouped[:], in_=w1_raw[b][:].rearrange("p j (q t) -> p t q j", t=PACK)[:, t0 : t0 + s1 - s0]
                 )
 
-            def prepare_w2(b):
-                raw = w2_raw[b]
-                for half in range(2):
-                    cols = slice(half * N // 2, (half + 1) * N // 2)
-                    grouped = early.tile([P, N // 2, PACK], BF16, name="w2_grouped", align_bytes=64, bufs=2)
-                    nc.scalar.copy(out=grouped[:], in_=raw[:, :, cols].rearrange("p t n -> p n t"))
-                    nc.vector.quantize_mx(
-                        out=w2_c[b][:, cols].bitcast(FP8X4), scales=w2_s[b][:, cols], in_=grouped[:].rearrange("p n t -> p (n t)")
-                    )
+            def quantize_w1(s0, s1, grouped):
+                b, t0 = divmod(s0, PACK)
+                nc.vector.quantize_mx(
+                    out=w1_c[b][:, P * t0 : P * (t0 + s1 - s0)].bitcast(FP8X4),
+                    scales=w1_s[:, P * s0 : P * s1],
+                    in_=grouped[:].rearrange("p t q j -> p (t q j)"),
+                )
+
+            def load_w2():
+                raw = early.tile([P, PASSES, PACK, N], F32, name="w2_raw", tag="w1_raw1")
+                for b in range(PASSES):
+                    nc.sync.dma_start(out=raw[:, b], in_=w2[512 * b : 512 * (b + 1), :].rearrange("(p t) n -> p t n", t=PACK))
+                return raw
+
+            def group_w2(raw, s):
+                b, half = divmod(s - 2, 2)
+                cols = slice(half * N // 2, (half + 1) * N // 2)
+                grouped = keep.tile([P, N // 2, PACK], BF16, name="w2_grouped", tag="factor%d" % s, align_bytes=64)
+                nc.scalar.copy(out=grouped[:], in_=raw[:, b, :, cols].rearrange("p t n -> p n t"))
+                return b, cols, grouped
 
             def stronger(s):
                 b, t = divmod(s, PACK)
                 strong = ring.tile([P, S], F32, name="strong", bufs=1)
                 for half in range(S // BANK):
                     cols = slice(half * BANK, (half + 1) * BANK)
-                    d1 = psum.tile([P, BANK], F32, name="d1", bufs=2)
-                    d2 = psum.tile([P, BANK], F32, name="d2", bufs=2)
+                    d1 = psum.tile([P, BANK], F32, name="d1")
+                    d2 = psum.tile([P, BANK], F32, name="d2")
                     nc.tensor.matmul_mx(
                         out=d2[:],
                         lhsT=w4_c[b][:, 2 * P * t : 2 * P * (t + 1)].bitcast(FP4X4),
@@ -156,22 +166,25 @@ def tile_list_tank_floor_repair_kernel(
                     )
                     nc.tensor.matmul_mx(
                         out=d1[:],
-                        lhsT=w1_c[s][:].bitcast(FP8X4),
-                        lhsT_scale=w1_s[s][:],
+                        lhsT=w1_c[b][:, P * t : P * (t + 1)].bitcast(FP8X4),
+                        lhsT_scale=w1_s[:, P * s : P * (s + 1)],
                         rhs=v_w[:, cols].bitcast(FP8X4),
                         rhs_scale=v_s[:, cols],
                         start=True,
                         stop=True,
                     )
-                    d2_sb = ring.tile([P, BANK], F32, name="d2_sb")
+                    d2_sb = ring.tile([P, BANK], F32, name="d2_sb", tag="d2_sb", align_bytes=64)
                     nc.scalar.copy(out=d2_sb[:], in_=d2[:])
                     nc.vector.tensor_tensor(out=strong[:, cols], in0=d1[:], in1=d2_sb[:], op=ALU.max)
-                factor = ring.tile([P, S], F32, name="factor")
-                nc.scalar.activation(out=factor[:], in_=wgs_t[t][:], func=COPY, scale=gains[:, b, t : t + 1])
+                factor = keep.tile([P, S], F32, name="factor", tag="factor%d" % s, align_bytes=64)
+                nc.scalar.activation(out=factor[:], in_=wgs_t[t][:], func=COPY, scale=gains[b][:, t : t + 1])
                 return strong, factor
 
             def fetch_before(s):
                 b, t = divmod(s, PACK)
+                if b == 0:
+                    nc.vector.tensor_copy(half_b[b][:, t, :], pages[s][:].indirect(idx4[:]))
+                    return
                 for half in range(2):
                     nc.vector.tensor_scalar(
                         half_b[b][:, t, 512 * half : 512 * (half + 1)],
@@ -182,86 +195,130 @@ def tile_list_tank_floor_repair_kernel(
                         ALU.add,
                     )
 
-            nc.vector.tensor_copy(v_s[:], tab_s[:].indirect(idx[:]))
-            nc.vector.tensor_copy(v_w[:], tab_w[:].indirect(idx[:]))
+            def fetch_rise(t):
+                nc.vector.tensor_tensor(rise[:, t, :], pages[t][:].indirect(idx3[:]), half_b[0][:, t, :], ALU.subtract)
+                nc.scalar.activation(out=rise[:, t, :], in_=rise[:, t, :], func=RELU, scale=2.0)
+
+            def sum_on_tensor(grouped):
+                for pair in range(4):
+                    words = psum.tile([P, 2, 2, P], F32, name="words")
+                    for k in range(2):
+                        m0 = 256 * pair + P * k
+                        turned = psum.tile([P, PACK, P], F32, name="turned")
+                        for t in range(PACK):
+                            nc.tensor.matmul(
+                                turned[:, t, :], rise[:, t, m0 : m0 + P], ident[:], start=True, stop=False, is_transpose=True
+                            )
+                            nc.tensor.matmul(
+                                turned[:, t, :], half_b[0][:, t, m0 : m0 + P], ident[:], start=False, stop=True, is_transpose=True
+                            )
+                        rounded = ring.tile([P, 2, P, 2], BF16, name="rounded")
+                        nc.scalar.copy(out=rounded[:], in_=turned[:].rearrange("m (u e) p -> m u p e", e=2))
+                        pairs = rounded[:].rearrange("m u p e -> m (u p e)").bitcast(F32)
+                        for u in range(2):
+                            nc.tensor.transpose(words[:, k, u, :], pairs[:, P * u : P * (u + 1)], ident[:])
+                    nc.scalar.copy(
+                        out=grouped[:, 256 * pair : 256 * (pair + 1), :]
+                        .rearrange("p m t -> p (m t)")
+                        .bitcast(F32)
+                        .rearrange("p (k m u) -> p k m u", k=2, u=2),
+                        in_=words[:].rearrange("p k u m -> p k m u"),
+                    )
+
             deal_w4(0)
-            fetch_before(0)
-            prepare_w1(0)
-            made = stronger(0)
-            for s in range(1, PACK):
-                prepare_w1(s)
             deal_w4(1)
+            make_identity(nc, ident[:])
+            fetch_before(0)
+            nc.vector.tensor_copy(v_w[:], tab_w[:].indirect(idx[:]))
+            nc.vector.tensor_copy(v_s[:], tab_s[:].indirect(idx[:]))
+            for s0 in (0, 2):
+                grouped = ring.tile([P, 2, P, PACK], BF16, name="w1_grouped", tag="d2_sb", align_bytes=64)
+                group_w1(s0, s0 + 2, grouped)
+                quantize_w1(s0, s0 + 2, grouped)
+            rise = early.tile([P, PACK, M], F32, name="rise", tag="tab_w")
+            made = stronger(0)
+            w2_pieces = []
             for s in range(SLICES):
                 strong, factor = made
                 nc.vector.tensor_tensor(pages[s][:].indirect(idx2[:]), strong[:], factor[:], ALU.mult)
+                if s == 1:
+                    w1_c.append(keep.tile([P, 512], U32, name="w1_c1", tag="factor1", align_bytes=64))
+                    quantize_w1(PACK, SLICES, w1_grouped)
+                if s < PACK:
+                    fetch_rise(s)
                 if s + 1 < SLICES:
                     made = stronger(s + 1)
                     fetch_before(s + 1)
+                if 2 <= s <= 5:
+                    w2_pieces.append(group_w2(w2_raw, s))
                 if s == 0:
-                    for later in range(PACK, SLICES):
-                        prepare_w1(later)
-                if s in (1, 2):
-                    prepare_w2(s - 1)
+                    w1_grouped = keep.tile([P, PACK, P, PACK], BF16, name="w1_grouped1", tag="factor0", align_bytes=64)
+                    group_w1(PACK, SLICES, w1_grouped)
+                    w2_raw = load_w2()
+                if s == PACK:
+                    x0_grouped = early.tile([P, M, PACK], BF16, name="x0_grouped", tag="w1_raw0", align_bytes=64)
+                    sum_on_tensor(x0_grouped)
+                if s == 6:
+                    w2_c = keep.tile([P, PASSES, N], U32, name="w2_c", tag="factor6", align_bytes=64)
+                    for b, cols, grouped in w2_pieces:
+                        nc.vector.quantize_mx(
+                            out=w2_c[:, b, cols].bitcast(FP8X4),
+                            scales=w2_s[b][:, cols],
+                            in_=grouped[:].rearrange("p n t -> p (n t)"),
+                        )
+            x0_c = keep.tile([P, M], U32, name="x0_c", tag="factor7", align_bytes=64)
+            nc.vector.quantize_mx(out=x0_c[:].bitcast(FP8X4), scales=x0_s[:], in_=x0_grouped[:].rearrange("p m t -> p (m t)"))
 
         late = ctx.enter_context(tc.tile_pool(name="late", bufs=2))
+        banks = ctx.enter_context(tc.psum_pool(name="banks", bufs=8))
         out_rows = out.rearrange("(c p) m -> p c m", p=P)
-        steps = []
-        start = 0
-        for width in PIECES:
-            for b in range(PASSES):
-                steps.append((start, width, b))
-            start += width
 
-        def combine(start, width, b):
+        def combine(start, width):
             diff = late.tile([P, PACK, width], F32, name="diff")
             for t in range(PACK):
                 nc.vector.tensor_tensor(
                     diff[:, t, :],
-                    pages[PACK * b + t][:].indirect(idx3[:, start // 16 : (start + width) // 16]),
-                    half_b[b][:, t, start : start + width],
+                    pages[PACK + t][:].indirect(idx3[:, start // 16 : (start + width) // 16]),
+                    half_b[1][:, t, start : start + width],
                     ALU.subtract,
                 )
-            nc.vector.tensor_tensor(out=diff[:], in0=diff[:], in1=half_b[b][:, :, start : start + width], op=ALU.max)
+            nc.vector.tensor_tensor(out=diff[:], in0=diff[:], in1=half_b[1][:, :, start : start + width], op=ALU.max)
             grouped = late.tile([P, width, PACK], BF16, name="x_grouped", align_bytes=64)
             nc.scalar.activation(out=grouped[:], in_=diff[:].rearrange("p t m -> p m t"), func=COPY, scale=2.0)
             return grouped
 
-        def quantize_x(width, grouped):
-            codes = late.tile([P, width], U32, name="x_c", align_bytes=64, bufs=4)
-            scales = late.tile([P, width], U8, name="x_s", align_bytes=64, bufs=4)
+        def score(start, width, grouped, last):
+            codes = late.tile([P, width], U32, name="x_c", align_bytes=64)
+            scales = late.tile([P, width], U8, name="x_s", align_bytes=64)
             nc.vector.quantize_mx(out=codes[:].bitcast(FP8X4), scales=scales[:], in_=grouped[:].rearrange("p m t -> p (m t)"))
-            return codes, scales
-
-        def score(start, width, operands, last):
+            operands = [(x0_c[:, start : start + width], x0_s[:, start : start + width]), (codes[:], scales[:])]
             per_bank = min(BANK // width, 3)
-            staged = late.tile([P, N // P, width], F32, name="staged")
-            for c0 in range(0, N // P, per_bank):
-                acc = psum.tile([P, per_bank, width], F32, name="acc", bufs=4)
-                for c in range(c0, c0 + per_bank):
-                    for b in range(PASSES):
-                        nc.tensor.matmul_mx(
-                            out=acc[:, c - c0, :],
-                            lhsT=w2_c[b][:, P * c : P * (c + 1)].bitcast(FP8X4),
-                            lhsT_scale=w2_s[b][:, P * c : P * (c + 1)],
-                            rhs=operands[b][0][:].bitcast(FP8X4),
-                            rhs_scale=operands[b][1][:],
-                            start=(b == 0),
-                            stop=(b == PASSES - 1),
-                        )
-                if last and (c0 // per_bank) % 2 == 1:
-                    nc.vector.tensor_copy(out=staged[:, c0 : c0 + per_bank, :], in_=acc[:])
+            accs = [banks.tile([P, per_bank, width], F32, name="acc") for c0 in range(0, N // P, per_bank)]
+            for b in range(PASSES):
+                for c in range(N // P):
+                    nc.tensor.matmul_mx(
+                        out=accs[c // per_bank][:, c % per_bank, :],
+                        lhsT=w2_c[:, b, P * c : P * (c + 1)].bitcast(FP8X4),
+                        lhsT_scale=w2_s[b][:, P * c : P * (c + 1)],
+                        rhs=operands[b][0].bitcast(FP8X4),
+                        rhs_scale=operands[b][1],
+                        start=(b == 0 and c % per_bank == 0),
+                        stop=(b == PASSES - 1 and c % per_bank == per_bank - 1),
+                    )
+            for i, acc in enumerate(accs):
+                staged = late.tile([P, per_bank, width], F32, name="staged", bufs=6)
+                if last and i % 2 == 1:
+                    nc.vector.tensor_copy(out=staged[:], in_=acc[:])
                 else:
-                    nc.scalar.copy(out=staged[:, c0 : c0 + per_bank, :], in_=acc[:])
-                nc.sync.dma_start(out=out_rows[:, c0 : c0 + per_bank, start : start + width], in_=staged[:, c0 : c0 + per_bank, :])
+                    nc.scalar.copy(out=staged[:], in_=acc[:])
+                nc.sync.dma_start(out=out_rows[:, per_bank * i : per_bank * (i + 1), start : start + width], in_=staged[:])
 
-        operands = []
         waiting = None
-        for step in steps + [None]:
-            grouped = combine(*step) if step is not None else None
+        start = 0
+        for width in PIECES:
+            grouped = combine(start, width)
             if waiting is not None:
-                (w_start, w_width, w_b), w_grouped = waiting
-                operands.append(quantize_x(w_width, w_grouped))
-                if w_b == PASSES - 1:
-                    score(w_start, w_width, operands, step is None)
-                    operands = []
-            waiting = (step, grouped)
+                score(*waiting, False)
+            waiting = (start, width, grouped)
+            start += width
+        score(*waiting, True)

from contextlib import ExitStack

import concourse.mybir as mybir
from concourse.masks import make_identity

K, T, S, T2, M, H, N = 512, 4096, 1024, 2048, 1024, 1024, 768
FLOPS = 2 * (2 * K * H * S + H * N * M)

F32 = mybir.dt.float32
BF16 = mybir.dt.bfloat16
I32 = mybir.dt.int32
U32 = mybir.dt.uint32
U16 = mybir.dt.uint16
U8 = mybir.dt.uint8
FP8X4 = mybir.dt.float8_e4m3fn_x4
FP4X4 = mybir.dt.float4_e2m1fn_x4
ALU = mybir.AluOpType
COPY = mybir.ActivationFunctionType.Copy
RELU = mybir.ActivationFunctionType.Relu

P = 128
PACK = 4
PASSES = H // (P * PACK)
SLICES = PASSES * PACK
BANK = 512
PIECES = (256, 256, 256, 128, 128)


def tile_list_tank_floor_repair_kernel(
    tc, tab_words, tab_scales, offs, w1, w4_words, w4_scales, gain, page0, wgs, offs2, offs3, offs4, w2, out
):
    nc = tc.nc
    with ExitStack() as ctx:
        lists = ctx.enter_context(tc.tile_pool(name="lists", bufs=1))
        keep = ctx.enter_context(tc.tile_pool(name="keep", bufs=1))
        ring = ctx.enter_context(tc.tile_pool(name="ring", bufs=2))
        with tc.tile_pool(name="early", bufs=1) as early, tc.psum_pool(name="psum", bufs=2) as psum:

            idx = lists.tile([P, S // 16], U16, name="idx")
            idx2 = lists.tile([P, S // 16], U16, name="idx2")
            idx3 = lists.tile([P, M // 16], U16, name="idx3")
            idx4 = lists.tile([P, M // 16], U16, name="idx4")

            tab_w = early.tile([P, T], U32, name="tab_w", tag="tab_w")
            tab_s = early.tile([P, T], U8, name="tab_s")
            w4_raw = [early.tile([P, H], U8, name="w4_raw%d" % b) for b in range(PASSES)]
            w4s_raw = early.tile([P, H], U8, name="w4s_raw")
            w1_raw = [early.tile([P, PACK, 512], F32, name="w1_raw%d" % b, tag="w1_raw%d" % b, align_bytes=64 if b == 0 else None) for b in range(PASSES)]
            ident = early.tile([P, P], F32, name="ident")
            x0_s = keep.tile([P, M], U8, name="x0_s", align_bytes=64)

            v_w = keep.tile([P, S], U32, name="v_w", align_bytes=64)
            v_s = keep.tile([P, S], U8, name="v_s", align_bytes=64)
            w4_c = [keep.tile([P, PACK * 2 * P], U8, name="w4_c%d" % b, align_bytes=64) for b in range(PASSES)]
            w4_s = [keep.tile([P, PACK * P], U8, name="w4_s%d" % b, align_bytes=64) for b in range(PASSES)]
            w1_c = [keep.tile([P, 512], U32, name="w1_c0", align_bytes=64)]
            w1_s = keep.tile([P, H], U8, name="w1_s", align_bytes=64)
            w2_s = [keep.tile([P, N], U8, name="w2_s%d" % b, align_bytes=64) for b in range(PASSES)]
            gains = [keep.tile([P, PACK], F32, name="gains%d" % b) for b in range(PASSES)]
            wgs_t = [keep.tile([P, S], F32, name="wgs_t%d" % t) for t in range(PACK)]
            pages = [keep.tile([P, T2], F32, name="page%d" % s) for s in range(SLICES)]
            half_b = [keep.tile([P, PACK, M], F32, name="half_b%d" % b) for b in range(PASSES)]

            page_rows = page0.rearrange("(b p t) c -> b t p c", p=P, t=PACK)
            wgs_rows = wgs.rearrange("(q t) j -> t q j", t=PACK)

            def load_page(s):
                nc.sync.dma_start(out=pages[s][:], in_=page_rows[s // PACK, s % PACK])

            def load_wgs(t):
                for quad in (0, 2, 1, 3):
                    nc.sync.dma_start(out=wgs_t[t][32 * quad : 32 * quad + 32, :], in_=wgs_rows[t])

            def load_gain(b):
                nc.sync.dma_start(out=gains[b][:], in_=gain[512 * b : 512 * (b + 1)].rearrange("(p t) -> p t", t=PACK))

            def load_w1(b):
                nc.sync.dma_start(out=w1_raw[b][:], in_=w1[:, 512 * b : 512 * (b + 1)].rearrange("(p j) c -> p j c", j=PACK))

            nc.vector.memset(tab_s[:].bitcast(I32), 0)
            nc.gpsimd.memset(w4s_raw[:].bitcast(I32), 0)
            nc.sync.dma_start(idx4[:], offs4)
            nc.sync.dma_start(idx[:], offs)
            nc.sync.dma_start(idx2[:], offs2)
            nc.sync.dma_start(idx3[:], offs3)
            load_gain(0)
            for b in range(PASSES):
                nc.sync.dma_start(out=w4_raw[b][:].bitcast(I32), in_=w4_words[0, :, H * b : H * (b + 1)].bitcast(I32))
            load_page(0)
            nc.sync.dma_start(out=tab_w[:].bitcast(I32), in_=tab_words[0].rearrange("p n i -> p (n i)").bitcast(I32))
            for quad in range(4):
                nc.sync.dma_start(
                    out=tab_s[32 * quad : 32 * quad + 4, :].bitcast(I32),
                    in_=tab_scales[0, 4 * quad : 4 * quad + 4, :].bitcast(I32),
                )
            for quad in range(4):
                nc.gpsimd.dma_start(
                    out=w4s_raw[32 * quad : 32 * quad + 4, :].bitcast(I32),
                    in_=w4_scales[0, 4 * quad : 4 * quad + 4, :].bitcast(I32),
                )
            load_w1(0)
            load_wgs(0)
            load_page(1)
            load_wgs(1)
            load_wgs(2)
            load_wgs(3)
            load_page(2)
            load_gain(1)
            load_page(3)
            load_w1(1)
            for s in range(PACK, SLICES):
                load_page(s)

            def deal_w4(b):
                nc.vector.tensor_copy(
                    out=w4_c[b][:].bitcast(U16).rearrange("p (t q) -> p t q", t=PACK),
                    in_=w4_raw[b][:].bitcast(U16).rearrange("p (q t) -> p t q", t=PACK),
                )
                nc.gpsimd.tensor_copy(
                    out=w4_s[b][:].rearrange("p (t q) -> p t q", t=PACK),
                    in_=w4s_raw[:, 512 * b : 512 * (b + 1)].rearrange("p (q t) -> p t q", t=PACK),
                )

            def group_w1(s0, s1, grouped):
                b, t0 = divmod(s0, PACK)
                nc.scalar.copy(
                    out=grouped[:], in_=w1_raw[b][:].rearrange("p j (q t) -> p t q j", t=PACK)[:, t0 : t0 + s1 - s0]
                )

            def quantize_w1(s0, s1, grouped):
                b, t0 = divmod(s0, PACK)
                nc.vector.quantize_mx(
                    out=w1_c[b][:, P * t0 : P * (t0 + s1 - s0)].bitcast(FP8X4),
                    scales=w1_s[:, P * s0 : P * s1],
                    in_=grouped[:].rearrange("p t q j -> p (t q j)"),
                )

            def load_w2():
                raw = early.tile([P, PASSES, PACK, N], F32, name="w2_raw", tag="w1_raw1")
                for b in range(PASSES):
                    nc.sync.dma_start(out=raw[:, b], in_=w2[512 * b : 512 * (b + 1), :].rearrange("(p t) n -> p t n", t=PACK))
                return raw

            def group_w2(raw, s):
                b, half = divmod(s - 2, 2)
                cols = slice(half * N // 2, (half + 1) * N // 2)
                grouped = keep.tile([P, N // 2, PACK], BF16, name="w2_grouped", tag="factor%d" % s, align_bytes=64)
                nc.scalar.copy(out=grouped[:], in_=raw[:, b, :, cols].rearrange("p t n -> p n t"))
                return b, cols, grouped

            def stronger(s):
                b, t = divmod(s, PACK)
                strong = ring.tile([P, S], F32, name="strong", bufs=1)
                for half in range(S // BANK):
                    cols = slice(half * BANK, (half + 1) * BANK)
                    d1 = psum.tile([P, BANK], F32, name="d1")
                    d2 = psum.tile([P, BANK], F32, name="d2")
                    nc.tensor.matmul_mx(
                        out=d2[:],
                        lhsT=w4_c[b][:, 2 * P * t : 2 * P * (t + 1)].bitcast(FP4X4),
                        lhsT_scale=w4_s[b][:, P * t : P * (t + 1)],
                        rhs=v_w[:, cols].bitcast(FP8X4),
                        rhs_scale=v_s[:, cols],
                        start=True,
                        stop=True,
                    )
                    nc.tensor.matmul_mx(
                        out=d1[:],
                        lhsT=w1_c[b][:, P * t : P * (t + 1)].bitcast(FP8X4),
                        lhsT_scale=w1_s[:, P * s : P * (s + 1)],
                        rhs=v_w[:, cols].bitcast(FP8X4),
                        rhs_scale=v_s[:, cols],
                        start=True,
                        stop=True,
                    )
                    d2_sb = ring.tile([P, BANK], F32, name="d2_sb", tag="d2_sb", align_bytes=64)
                    nc.scalar.copy(out=d2_sb[:], in_=d2[:])
                    nc.vector.tensor_tensor(out=strong[:, cols], in0=d1[:], in1=d2_sb[:], op=ALU.max)
                factor = keep.tile([P, S], F32, name="factor", tag="factor%d" % s, align_bytes=64)
                nc.scalar.activation(out=factor[:], in_=wgs_t[t][:], func=COPY, scale=gains[b][:, t : t + 1])
                return strong, factor

            def fetch_before(s):
                b, t = divmod(s, PACK)
                if b == 0:
                    nc.vector.tensor_copy(half_b[b][:, t, :], pages[s][:].indirect(idx4[:]))
                    return
                for half in range(2):
                    nc.vector.tensor_scalar(
                        half_b[b][:, t, 512 * half : 512 * (half + 1)],
                        pages[s][:].indirect(idx4[:, 32 * half : 32 * (half + 1)]),
                        0.5,
                        0.0,
                        ALU.mult,
                        ALU.add,
                    )

            def fetch_rise(t):
                nc.vector.tensor_tensor(rise[:, t, :], pages[t][:].indirect(idx3[:]), half_b[0][:, t, :], ALU.subtract)
                nc.scalar.activation(out=rise[:, t, :], in_=rise[:, t, :], func=RELU, scale=2.0)

            def sum_on_tensor(grouped):
                for pair in range(4):
                    words = psum.tile([P, 2, 2, P], F32, name="words")
                    for k in range(2):
                        m0 = 256 * pair + P * k
                        turned = psum.tile([P, PACK, P], F32, name="turned")
                        for t in range(PACK):
                            nc.tensor.matmul(
                                turned[:, t, :], rise[:, t, m0 : m0 + P], ident[:], start=True, stop=False, is_transpose=True
                            )
                            nc.tensor.matmul(
                                turned[:, t, :], half_b[0][:, t, m0 : m0 + P], ident[:], start=False, stop=True, is_transpose=True
                            )
                        rounded = ring.tile([P, 2, P, 2], BF16, name="rounded")
                        nc.scalar.copy(out=rounded[:], in_=turned[:].rearrange("m (u e) p -> m u p e", e=2))
                        pairs = rounded[:].rearrange("m u p e -> m (u p e)").bitcast(F32)
                        for u in range(2):
                            nc.tensor.transpose(words[:, k, u, :], pairs[:, P * u : P * (u + 1)], ident[:])
                    nc.scalar.copy(
                        out=grouped[:, 256 * pair : 256 * (pair + 1), :]
                        .rearrange("p m t -> p (m t)")
                        .bitcast(F32)
                        .rearrange("p (k m u) -> p k m u", k=2, u=2),
                        in_=words[:].rearrange("p k u m -> p k m u"),
                    )

            deal_w4(0)
            deal_w4(1)
            make_identity(nc, ident[:])
            fetch_before(0)
            nc.vector.tensor_copy(v_w[:], tab_w[:].indirect(idx[:]))
            nc.vector.tensor_copy(v_s[:], tab_s[:].indirect(idx[:]))
            for s0 in (0, 2):
                grouped = ring.tile([P, 2, P, PACK], BF16, name="w1_grouped", tag="d2_sb", align_bytes=64)
                group_w1(s0, s0 + 2, grouped)
                quantize_w1(s0, s0 + 2, grouped)
            rise = early.tile([P, PACK, M], F32, name="rise", tag="tab_w")
            made = stronger(0)
            w2_pieces = []
            for s in range(SLICES):
                strong, factor = made
                nc.vector.tensor_tensor(pages[s][:].indirect(idx2[:]), strong[:], factor[:], ALU.mult)
                if s == 1:
                    w1_c.append(keep.tile([P, 512], U32, name="w1_c1", tag="factor1", align_bytes=64))
                    quantize_w1(PACK, SLICES, w1_grouped)
                if s < PACK:
                    fetch_rise(s)
                if s + 1 < SLICES:
                    made = stronger(s + 1)
                    fetch_before(s + 1)
                if 2 <= s <= 5:
                    w2_pieces.append(group_w2(w2_raw, s))
                if s == 0:
                    w1_grouped = keep.tile([P, PACK, P, PACK], BF16, name="w1_grouped1", tag="factor0", align_bytes=64)
                    group_w1(PACK, SLICES, w1_grouped)
                    w2_raw = load_w2()
                if s == PACK:
                    x0_grouped = early.tile([P, M, PACK], BF16, name="x0_grouped", tag="w1_raw0", align_bytes=64)
                    sum_on_tensor(x0_grouped)
                if s == 6:
                    w2_c = keep.tile([P, PASSES, N], U32, name="w2_c", tag="factor6", align_bytes=64)
                    for b, cols, grouped in w2_pieces:
                        nc.vector.quantize_mx(
                            out=w2_c[:, b, cols].bitcast(FP8X4),
                            scales=w2_s[b][:, cols],
                            in_=grouped[:].rearrange("p n t -> p (n t)"),
                        )
            x0_c = keep.tile([P, M], U32, name="x0_c", tag="factor7", align_bytes=64)
            nc.vector.quantize_mx(out=x0_c[:].bitcast(FP8X4), scales=x0_s[:], in_=x0_grouped[:].rearrange("p m t -> p (m t)"))

        late = ctx.enter_context(tc.tile_pool(name="late", bufs=2))
        banks = ctx.enter_context(tc.psum_pool(name="banks", bufs=8))
        out_rows = out.rearrange("(c p) m -> p c m", p=P)

        def combine(start, width):
            diff = late.tile([P, PACK, width], F32, name="diff")
            for t in range(PACK):
                nc.vector.tensor_tensor(
                    diff[:, t, :],
                    pages[PACK + t][:].indirect(idx3[:, start // 16 : (start + width) // 16]),
                    half_b[1][:, t, start : start + width],
                    ALU.subtract,
                )
            nc.vector.tensor_tensor(out=diff[:], in0=diff[:], in1=half_b[1][:, :, start : start + width], op=ALU.max)
            grouped = late.tile([P, width, PACK], BF16, name="x_grouped", align_bytes=64)
            nc.scalar.activation(out=grouped[:], in_=diff[:].rearrange("p t m -> p m t"), func=COPY, scale=2.0)
            return grouped

        def score(start, width, grouped, last):
            codes = late.tile([P, width], U32, name="x_c", align_bytes=64)
            scales = late.tile([P, width], U8, name="x_s", align_bytes=64)
            nc.vector.quantize_mx(out=codes[:].bitcast(FP8X4), scales=scales[:], in_=grouped[:].rearrange("p m t -> p (m t)"))
            operands = [(x0_c[:, start : start + width], x0_s[:, start : start + width]), (codes[:], scales[:])]
            per_bank = min(BANK // width, 3)
            accs = [banks.tile([P, per_bank, width], F32, name="acc") for c0 in range(0, N // P, per_bank)]
            for b in range(PASSES):
                for c in range(N // P):
                    nc.tensor.matmul_mx(
                        out=accs[c // per_bank][:, c % per_bank, :],
                        lhsT=w2_c[:, b, P * c : P * (c + 1)].bitcast(FP8X4),
                        lhsT_scale=w2_s[b][:, P * c : P * (c + 1)],
                        rhs=operands[b][0].bitcast(FP8X4),
                        rhs_scale=operands[b][1],
                        start=(b == 0 and c % per_bank == 0),
                        stop=(b == PASSES - 1 and c % per_bank == per_bank - 1),
                    )
            for i, acc in enumerate(accs):
                staged = late.tile([P, per_bank, width], F32, name="staged", bufs=6)
                if last and i % 2 == 1:
                    nc.vector.tensor_copy(out=staged[:], in_=acc[:])
                else:
                    nc.scalar.copy(out=staged[:], in_=acc[:])
                nc.sync.dma_start(out=out_rows[:, per_bank * i : per_bank * (i + 1), start : start + width], in_=staged[:])

        waiting = None
        start = 0
        for width in PIECES:
            grouped = combine(start, width)
            if waiting is not None:
                score(*waiting, False)
            waiting = (start, width, grouped)
            start += width
        score(*waiting, True)
